import numpy as np
import ml_dtypes


def mxq(x, axis, fmt="e4m3"):
    dtype, down = {"e4m3": (ml_dtypes.float8_e4m3fn, 7), "e5m2": (ml_dtypes.float8_e5m2, 14)}[fmt]
    v = np.moveaxis(np.asarray(x, np.float32).astype(ml_dtypes.bfloat16).astype(np.float64), axis, -1)
    blocks = v.reshape(v.shape[:-1] + (-1, 32))
    amax = np.abs(blocks).max(-1, keepdims=True)
    byte = np.maximum(np.where(amax > 0, np.frexp(amax)[1] - 1 + 127, 0) - down, 1)
    scale = np.exp2(byte - 127.0)
    codes = (blocks / scale).astype(np.float32).astype(dtype).astype(np.float64)
    return np.moveaxis((codes * scale).reshape(v.shape), -1, axis)


WIDE = False


def mx_kscale(k):
    if not WIDE:
        return np.ones(k)
    levels = np.array([10, -10, 5, -5, 0])
    if k % 512:
        return np.exp2(np.random.permutation(np.resize(levels, k // 32))).repeat(32)
    a = np.empty((k // 512, 16))
    for p in range(k // 512):
        a[p, :8] = np.random.permutation(np.resize(levels, 8))
        for g in range(8):
            far = levels[np.abs(levels - a[p, g]) >= 10]
            a[p, g + 8] = far[np.random.randint(len(far))]
    return np.exp2(a.ravel()).repeat(32)


def f64(x):
    return np.asarray(x).astype(np.float64)


E2M1 = np.array([0.0, 0.5, 1.0, 1.5, 2.0, 3.0, 4.0, 6.0, -0.0, -0.5, -1.0, -1.5, -2.0, -3.0, -4.0, -6.0])


def pack_weight(w, fmt):
    k, n = w.shape
    w = f64(np.asarray(w, np.float32).astype(ml_dtypes.bfloat16)).reshape(k // 32, 32, n)
    amax = np.abs(w).max(1)
    if fmt == "e4m3":
        byte = np.frexp(amax)[1] - 1 + 127 - 7
    else:
        mant, ex = np.frexp(amax / 6.0)
        byte = np.where(mant > 0.5, ex, ex - 1) + 127
    byte = np.clip(np.where(amax > 0, byte, 1), 1, 254)
    scaled = (w * np.exp2(127.0 - byte)[:, None, :]).reshape(k, n).astype(np.float32)
    by_word = np.ascontiguousarray(scaled.reshape(k // 512, 128, 4, n).transpose(0, 1, 3, 2))
    if fmt == "e4m3":
        words = by_word.astype(ml_dtypes.float8_e4m3fn).view(np.uint8)
    else:
        c = by_word.astype(ml_dtypes.float4_e2m1fn).view(np.uint8) & 0xF
        words = (c[..., 0::2] | (c[..., 1::2] << 4)).reshape(k // 512, 128, 2 * n)
    return np.ascontiguousarray(words), np.ascontiguousarray(byte.astype(np.uint8).reshape(k // 512, 16, n))


def unpack_weight(words, scales, fmt):
    g, _, n = scales.shape
    words = np.ascontiguousarray(words).reshape(g, 128, n, -1)
    if fmt == "e4m3":
        vals = words.view(ml_dtypes.float8_e4m3fn).astype(np.float64)
    else:
        nib = np.empty((g, 128, n, 4), np.uint8)
        nib[..., 0::2] = words & 0xF
        nib[..., 1::2] = words >> 4
        vals = E2M1[nib]
    vals = vals * np.repeat(np.exp2(scales.astype(np.float64) - 127.0), 8, axis=1)[..., None]
    return vals.transpose(0, 1, 3, 2).reshape(g * 512, n)


def silu(v):
    return v / (1.0 + np.exp(-np.maximum(v, -700.0)))


D, K, M, T = 64, 1536, 512, 512


def setup_inputs():
    n = np.random.standard_normal
    s = mx_kscale(K)[:, None]
    p_w0 = pack_weight(n((K, M)) / np.sqrt(K) / s, "e2m1")
    p_w1 = pack_weight(n((K, M)) / np.sqrt(K) / s, "e4m3")
    return {
        "x": (n((K, T + 2 * D)) * s).astype(np.float32),
        "w0_words": p_w0[0],
        "w0_scales": p_w0[1],
        "w1_words": p_w1[0],
        "w1_scales": p_w1[1],
        "w2": (n((K, M)) / np.sqrt(K) / s).astype(np.float32),
        "b": (0.3 * n(512)).astype(np.float32),
    }


def reference(x, w0_words, w0_scales, w1_words, w1_scales, w2, b):
    x_ = mxq(f64(x), 0, "e4m3")
    w0_ = unpack_weight(w0_words, w0_scales, "e2m1")
    w1_ = unpack_weight(w1_words, w1_scales, "e4m3")
    w2_ = mxq(f64(w2), 0, "e4m3")
    y = x_[:, :T].T @ w0_ + x_[:, D:D + T].T @ w1_ + x_[:, 2 * D:].T @ w2_
    return silu(y + f64(b)[None, :])

@@ -1,0 +1,202 @@
+from contextlib import ExitStack
+
+import concourse.mybir as mybir
+from concourse.masks import make_identity
+
+D, K, M, T = 64, 1536, 512, 512
+FLOPS = 2 * 3 * K * M * T
+
+F32 = mybir.dt.float32
+BF16 = mybir.dt.bfloat16
+I32 = mybir.dt.int32
+U32 = mybir.dt.uint32
+U8 = mybir.dt.uint8
+FP8X4 = mybir.dt.float8_e4m3fn_x4
+FP4X4 = mybir.dt.float4_e2m1fn_x4
+SILU = mybir.ActivationFunctionType.Silu
+ADD = mybir.AluOpType.add
+
+P = 128
+PACK = 4
+K_PASS = P * PACK
+PASSES = K // K_PASS
+XW = T + 2 * D
+TILES = T // P
+HALF = M // 2
+N_FP4 = 128
+X_CHUNKS = ((0, 256), (256, 384), (384, 640))
+W2_VECTOR_COLS = 128
+
+
+def interleave(copy, grouped, raw, c0, c1):
+    dst = grouped[:, PACK * c0 : PACK * c1].rearrange("p (c i t) -> p c t i", i=4, t=PACK)
+    src = raw[:, :, c0:c1].rearrange("p t (c i) -> p c t i", i=4)
+    copy(out=dst, in_=src)
+
+
+def tile_mix_dconv_tm_silu_kernel(tc, x, w0_words, w0_scales, w1_words, w1_scales, w2, b, out):
+    nc = tc.nc
+    with ExitStack() as ctx:
+        keep = ctx.enter_context(tc.tile_pool(name="keep", bufs=1))
+        psum = ctx.enter_context(tc.psum_pool(name="psum", bufs=1))
+        ctx.enter_context(tc.manual_schedule())
+
+        b_col = keep.tile([P, PACK], F32, name="b_col")
+        nc.scalar.dma_start(out=b_col[:], in_=b.rearrange("(p c) -> p c", c=PACK))
+
+        x_raw = [keep.tile([P, PACK, XW], F32, name="x_raw%d" % a) for a in range(PASSES)]
+        w2_raw = {}
+        for h in range(2):
+            for a in range(PASSES):
+                w2_raw[h, a] = keep.tile([P, PACK, HALF], F32, name="w2_raw%d%d" % (h, a))
+        w0_codes = keep.tile([P, PASSES * 2 * M], U8, name="w0_codes", align_bytes=64)
+        w1_codes = keep.tile([P, PASSES * M], U32, name="w1_codes", align_bytes=64)
+        w0_plane = keep.tile([P, PASSES * M], U8, name="w0_plane", align_bytes=64)
+        w1_plane = keep.tile([P, PASSES * M], U8, name="w1_plane", align_bytes=64)
+
+        def rows(t, a):
+            return t[a * K_PASS : (a + 1) * K_PASS, :].rearrange("(p j) w -> p j w", j=PACK)
+
+        def load_scales(plane, scales):
+            nc.vector.memset(plane[:].bitcast(I32), 0)
+            by_row = scales.bitcast(I32).rearrange("a (q r) n -> r q a n", r=4)
+            for r in range(4):
+                nc.sync.dma_start(
+                    out=plane[r:P:32, :].bitcast(I32).rearrange("q (a n) -> q a n", a=PASSES),
+                    in_=by_row[r],
+                )
+
+        nc.sync.dma_start(out=x_raw[0][:], in_=rows(x, 0))
+        nc.sync.dma_start(
+            out=w1_codes[:].bitcast(I32).rearrange("p (a n) -> p a n", a=PASSES),
+            in_=w1_words.rearrange("a p n t -> p a (n t)").bitcast(I32),
+        )
+        load_scales(w1_plane, w1_scales)
+        nc.sync.dma_start(
+            out=w0_codes[:].bitcast(I32).rearrange("p (a n) -> p a n", a=PASSES),
+            in_=w0_words.rearrange("a p n -> p a n").bitcast(I32),
+        )
+        nc.sync.dma_start(out=x_raw[1][:], in_=rows(x, 1))
+        load_scales(w0_plane, w0_scales)
+        nc.sync.dma_start(out=x_raw[2][:], in_=rows(x, 2))
+        for h in range(2):
+            for a in range(PASSES):
+                nc.sync.dma_start(out=w2_raw[h, a][:], in_=rows(w2, a)[:, :, h * HALF : (h + 1) * HALF])
+
+        ident = keep.tile([P, P], F32, name="ident")
+        make_identity(nc, ident[:])
+        warm = keep.tile([P, 8], F32, name="warm")
+        nc.scalar.activation(out=warm[:], in_=ident[:, 0:8], func=SILU)
+
+        spread = psum.tile([P, PACK, P], F32, name="spread", tag="bank7")
+        for c in range(PACK):
+            nc.tensor.transpose(spread[:, c, :], b_col[:, c : c + 1].to_broadcast([P, P]), ident[:])
+        bias = keep.tile([P, M], F32, name="bias")
+        nc.scalar.copy(out=bias[:].rearrange("j (p c) -> j p c", c=PACK), in_=spread[:].rearrange("j c p -> j p c"))
+
+        acc = {}
+        for h in range(2):
+            for m in range(TILES):
+                acc[h, m] = psum.tile([P, HALF], F32, name="acc%d%d" % (h, m), tag="bank%d" % (h * TILES + m))
+
+        x_codes = [keep.tile([P, XW], U32, name="x_codes%d" % a, align_bytes=64) for a in range(PASSES)]
+        x_plane = [keep.tile([P, XW], U8, name="x_plane%d" % a, align_bytes=64) for a in range(PASSES)]
+
+        def quantize(codes, plane, grouped, c0, c1):
+            nc.vector.quantize_mx(
+                out=codes[:, c0:c1].bitcast(FP8X4), scales=plane[:, c0:c1], in_=grouped[:, PACK * c0 : PACK * c1]
+            )
+
+        def prepare_x(a):
+            grouped = keep.tile([P, PACK * XW], BF16, name="x_grouped%d" % a, align_bytes=64)
+            interleave(nc.vector.tensor_copy, grouped, x_raw[a], *X_CHUNKS[0])
+            interleave(nc.vector.tensor_copy, grouped, x_raw[a], *X_CHUNKS[1])
+            interleave(nc.scalar.copy, grouped, x_raw[a], *X_CHUNKS[2])
+            for c0, c1 in X_CHUNKS:
+                quantize(x_codes[a], x_plane[a], grouped, c0, c1)
+
+        def product(h, m, a, tap, cols, rhs, rhs_scale, start=False, stop=False):
+            t0 = tap * D + m * P
+            nc.tensor.matmul_mx(
+                out=acc[h, m][:, cols],
+                lhsT=x_codes[a][:, t0 : t0 + P].bitcast(FP8X4),
+                lhsT_scale=x_plane[a][:, t0 : t0 + P],
+                rhs=rhs,
+                rhs_scale=rhs_scale,
+                start=start,
+                stop=stop,
+            )
+
+        def packed_taps(a, halves):
+            for m in range(TILES):
+                for h in halves:
+                    n0 = a * M + h * HALF
+                    product(h, m, a, 1, slice(0, HALF), w1_codes[:, n0 : n0 + HALF].bitcast(FP8X4),
+                            w1_plane[:, n0 : n0 + HALF], start=(a == 0))
+            for m in range(TILES):
+                for h in halves:
+                    for q in range(0, HALF, N_FP4):
+                        n0 = a * M + h * HALF + q
+                        product(h, m, a, 0, slice(q, q + N_FP4),
+                                w0_codes[:, 2 * n0 : 2 * (n0 + N_FP4)].bitcast(FP4X4), w0_plane[:, n0 : n0 + N_FP4])
+
+        w2_grouped, w2_codes, w2_plane = {}, {}, {}
+
+        def cast_w2(h, a):
+            g = keep.tile([P, PACK * HALF], BF16, name="w2_grouped%d%d" % (h, a), align_bytes=64)
+            w2_grouped[h, a] = g
+            interleave(nc.vector.tensor_copy, g, w2_raw[h, a], 0, W2_VECTOR_COLS)
+            interleave(nc.scalar.copy, g, w2_raw[h, a], W2_VECTOR_COLS, HALF)
+
+        def finish_w2(h, a):
+            codes = keep.tile([P, HALF], U32, name="w2_codes%d%d" % (h, a), align_bytes=64)
+            plane = keep.tile([P, HALF], U8, name="w2_plane%d%d" % (h, a), align_bytes=64)
+            quantize(codes, plane, w2_grouped[h, a], 0, HALF)
+            for m in range(TILES):
+                product(h, m, a, 2, slice(0, HALF), codes[:].bitcast(FP8X4), plane[:], stop=(a == PASSES - 1))
+
+        pre = {}
+        res = [keep.tile([P, TILES, HALF], F32, name="res%d" % h) for h in range(2)]
+        out_tiles = out.rearrange("(m p) n -> p m n", p=P)
+
+        def add_bias(h, m):
+            s = keep.tile([P, HALF], F32, name="pre%d%d" % (h, m))
+            pre[h, m] = s
+            nc.vector.tensor_tensor(out=s[:], in0=acc[h, m][:], in1=bias[:, h * HALF : (h + 1) * HALF], op=ADD)
+
+        def silu(h, m):
+            nc.scalar.activation(out=res[h][:, m, :], in_=pre[h, m][:], func=SILU)
+
+        def store(h, m0, m1):
+            nc.sync.dma_start(out=out_tiles[:, m0:m1, h * HALF : (h + 1) * HALF], in_=res[h][:, m0:m1, :])
+
+        for a in range(PASSES - 1):
+            prepare_x(a)
+            packed_taps(a, (0, 1))
+        prepare_x(PASSES - 1)
+        packed_taps(PASSES - 1, (0,))
+        for a in range(PASSES):
+            cast_w2(0, a)
+            finish_w2(0, a)
+        packed_taps(PASSES - 1, (1,))
+
+        cast_w2(1, 0)
+        add_bias(0, 0)
+        finish_w2(1, 0)
+        add_bias(0, 1)
+        silu(0, 0)
+        cast_w2(1, 1)
+        add_bias(0, 2)
+        finish_w2(1, 1)
+        silu(0, 1)
+        store(0, 0, 2)
+        cast_w2(1, 2)
+        add_bias(0, 3)
+        finish_w2(1, 2)
+        silu(0, 2)
+        silu(0, 3)
+        store(0, 2, 4)
+        for m in range(TILES):
+            add_bias(1, m)
+            silu(1, m)
+            store(1, m, m + 1)

@@ -25,7 +25,8 @@ TILES = T // P
 HALF = M // 2
 N_FP4 = 128
 X_CHUNKS = ((0, 256), (256, 384), (384, 640))
-W2_VECTOR_COLS = 128
+W2_VECTOR = ((0, 128), (128, 256), (256, 288))
+W2_SCALAR = ((288, 384), (384, 512))
 
 
 def interleave(copy, grouped, raw, c0, c1):
@@ -45,12 +46,9 @@ def tile_mix_dconv_tm_silu_kernel(tc, x, w0_words, w0_scales, w1_words, w1_scale
         nc.scalar.dma_start(out=b_col[:], in_=b.rearrange("(p c) -> p c", c=PACK))
 
         x_raw = [keep.tile([P, PACK, XW], F32, name="x_raw%d" % a) for a in range(PASSES)]
-        w2_raw = {}
-        for h in range(2):
-            for a in range(PASSES):
-                w2_raw[h, a] = keep.tile([P, PACK, HALF], F32, name="w2_raw%d%d" % (h, a))
+        w2_raw = [keep.tile([P, PACK, M], F32, name="w2_raw%d" % a) for a in range(PASSES)]
         w0_codes = keep.tile([P, PASSES * 2 * M], U8, name="w0_codes", align_bytes=64)
-        w1_codes = keep.tile([P, PASSES * M], U32, name="w1_codes", align_bytes=64)
+        w1_codes = [keep.tile([P, M], U32, name="w1_codes%d" % a, align_bytes=64) for a in range(PASSES)]
         w0_plane = keep.tile([P, PASSES * M], U8, name="w0_plane", align_bytes=64)
         w1_plane = keep.tile([P, PASSES * M], U8, name="w1_plane", align_bytes=64)
 
@@ -66,41 +64,47 @@ def tile_mix_dconv_tm_silu_kernel(tc, x, w0_words, w0_scales, w1_words, w1_scale
                     in_=by_row[r],
                 )
 
+        def load_w1(a):
+            nc.sync.dma_start(
+                out=w1_codes[a][:].bitcast(I32), in_=w1_words[a].rearrange("p n t -> p (n t)").bitcast(I32)
+            )
+
+        ident = keep.tile([P, P], F32, name="ident")
+        make_identity(nc, ident[:])
+
         nc.sync.dma_start(out=x_raw[0][:], in_=rows(x, 0))
-        nc.sync.dma_start(
-            out=w1_codes[:].bitcast(I32).rearrange("p (a n) -> p a n", a=PASSES),
-            in_=w1_words.rearrange("a p n t -> p a (n t)").bitcast(I32),
-        )
-        load_scales(w1_plane, w1_scales)
         nc.sync.dma_start(
             out=w0_codes[:].bitcast(I32).rearrange("p (a n) -> p a n", a=PASSES),
             in_=w0_words.rearrange("a p n -> p a n").bitcast(I32),
         )
-        nc.sync.dma_start(out=x_raw[1][:], in_=rows(x, 1))
         load_scales(w0_plane, w0_scales)
+        load_w1(0)
+        nc.sync.dma_start(out=x_raw[1][:], in_=rows(x, 1))
+        load_scales(w1_plane, w1_scales)
         nc.sync.dma_start(out=x_raw[2][:], in_=rows(x, 2))
-        for h in range(2):
-            for a in range(PASSES):
-                nc.sync.dma_start(out=w2_raw[h, a][:], in_=rows(w2, a)[:, :, h * HALF : (h + 1) * HALF])
+        for a in range(PASSES):
+            nc.sync.dma_start(out=w2_raw[a][:], in_=rows(w2, a))
+        for a in range(1, PASSES):
+            load_w1(a)
 
-        ident = keep.tile([P, P], F32, name="ident")
-        make_identity(nc, ident[:])
         warm = keep.tile([P, 8], F32, name="warm")
         nc.scalar.activation(out=warm[:], in_=ident[:, 0:8], func=SILU)
 
-        spread = psum.tile([P, PACK, P], F32, name="spread", tag="bank7")
+        spread = psum.tile([P, PACK, P], F32, name="spread")
         for c in range(PACK):
             nc.tensor.transpose(spread[:, c, :], b_col[:, c : c + 1].to_broadcast([P, P]), ident[:])
         bias = keep.tile([P, M], F32, name="bias")
         nc.scalar.copy(out=bias[:].rearrange("j (p c) -> j p c", c=PACK), in_=spread[:].rearrange("j c p -> j p c"))
 
+        pieces = [(m, 0, M) for m in range(TILES - 1)] + [(TILES - 1, 0, HALF), (TILES - 1, HALF, HALF)]
         acc = {}
-        for h in range(2):
-            for m in range(TILES):
-                acc[h, m] = psum.tile([P, HALF], F32, name="acc%d%d" % (h, m), tag="bank%d" % (h * TILES + m))
+        for pc in pieces:
+            acc[pc] = psum.tile([P, pc[2]], F32, name="acc%d_%d" % pc[:2])
 
         x_codes = [keep.tile([P, XW], U32, name="x_codes%d" % a, align_bytes=64) for a in range(PASSES)]
         x_plane = [keep.tile([P, XW], U8, name="x_plane%d" % a, align_bytes=64) for a in range(PASSES)]
+        w2_codes = [keep.tile([P, M], U32, name="w2_codes%d" % a, align_bytes=64) for a in range(PASSES)]
+        w2_plane = [keep.tile([P, M], U8, name="w2_plane%d" % a, align_bytes=64) for a in range(PASSES)]
 
         def quantize(codes, plane, grouped, c0, c1):
             nc.vector.quantize_mx(
@@ -115,88 +119,77 @@ def tile_mix_dconv_tm_silu_kernel(tc, x, w0_words, w0_scales, w1_words, w1_scale
             for c0, c1 in X_CHUNKS:
                 quantize(x_codes[a], x_plane[a], grouped, c0, c1)
 
-        def product(h, m, a, tap, cols, rhs, rhs_scale, start=False, stop=False):
+        def prepare_w2(a):
+            grouped = keep.tile([P, PACK * M], BF16, name="w2_grouped%d" % a, align_bytes=64)
+            for c0, c1 in W2_SCALAR:
+                interleave(nc.scalar.copy, grouped, w2_raw[a], c0, c1)
+            interleave(nc.vector.tensor_copy, grouped, w2_raw[a], *W2_VECTOR[0])
+            interleave(nc.vector.tensor_copy, grouped, w2_raw[a], *W2_VECTOR[1])
+            quantize(w2_codes[a], w2_plane[a], grouped, 0, 128)
+            interleave(nc.vector.tensor_copy, grouped, w2_raw[a], *W2_VECTOR[2])
+            for c0 in range(128, M, 128):
+                quantize(w2_codes[a], w2_plane[a], grouped, c0, c0 + 128)
+
+        def product(pc, a, tap, start=False, stop=False):
+            m, c0, width = pc
             t0 = tap * D + m * P
-            nc.tensor.matmul_mx(
-                out=acc[h, m][:, cols],
-                lhsT=x_codes[a][:, t0 : t0 + P].bitcast(FP8X4),
-                lhsT_scale=x_plane[a][:, t0 : t0 + P],
-                rhs=rhs,
-                rhs_scale=rhs_scale,
-                start=start,
-                stop=stop,
-            )
+            step = N_FP4 if tap == 0 and width < M else width
+            for q in range(0, width, step):
+                n0 = c0 + q
+                if tap == 0:
+                    rhs = w0_codes[:, 2 * (a * M + n0) : 2 * (a * M + n0 + step)].bitcast(FP4X4)
+                    rhs_scale = w0_plane[:, a * M + n0 : a * M + n0 + step]
+                elif tap == 1:
+                    rhs = w1_codes[a][:, n0 : n0 + step].bitcast(FP8X4)
+                    rhs_scale = w1_plane[:, a * M + n0 : a * M + n0 + step]
+                else:
+                    rhs = w2_codes[a][:, n0 : n0 + step].bitcast(FP8X4)
+                    rhs_scale = w2_plane[a][:, n0 : n0 + step]
+                nc.tensor.matmul_mx(
+                    out=acc[pc][:, q : q + step],
+                    lhsT=x_codes[a][:, t0 : t0 + P].bitcast(FP8X4),
+                    lhsT_scale=x_plane[a][:, t0 : t0 + P],
+                    rhs=rhs,
+                    rhs_scale=rhs_scale,
+                    start=start and q == 0,
+                    stop=stop,
+                )
 
-        def packed_taps(a, halves):
-            for m in range(TILES):
-                for h in halves:
-                    n0 = a * M + h * HALF
-                    product(h, m, a, 1, slice(0, HALF), w1_codes[:, n0 : n0 + HALF].bitcast(FP8X4),
-                            w1_plane[:, n0 : n0 + HALF], start=(a == 0))
-            for m in range(TILES):
-                for h in halves:
-                    for q in range(0, HALF, N_FP4):
-                        n0 = a * M + h * HALF + q
-                        product(h, m, a, 0, slice(q, q + N_FP4),
-                                w0_codes[:, 2 * n0 : 2 * (n0 + N_FP4)].bitcast(FP4X4), w0_plane[:, n0 : n0 + N_FP4])
+        def products(a, tap, start=False):
+            for pc in pieces:
+                product(pc, a, tap, start=start)
 
-        w2_grouped, w2_codes, w2_plane = {}, {}, {}
+        def finish(pc):
+            m, c0, width = pc
+            pre = keep.tile([P, width], F32, name="pre%d_%d" % pc[:2])
+            res = keep.tile([P, width], F32, name="res%d_%d" % pc[:2])
+            nc.vector.tensor_tensor(out=pre[:], in0=acc[pc][:], in1=bias[:, c0 : c0 + width], op=ADD)
+            nc.scalar.activation(out=res[:], in_=pre[:], func=SILU)
+            nc.sync.dma_start(out=out[m * P : (m + 1) * P, c0 : c0 + width], in_=res[:])
 
-        def cast_w2(h, a):
-            g = keep.tile([P, PACK * HALF], BF16, name="w2_grouped%d%d" % (h, a), align_bytes=64)
-            w2_grouped[h, a] = g
-            interleave(nc.vector.tensor_copy, g, w2_raw[h, a], 0, W2_VECTOR_COLS)
-            interleave(nc.scalar.copy, g, w2_raw[h, a], W2_VECTOR_COLS, HALF)
-
-        def finish_w2(h, a):
-            codes = keep.tile([P, HALF], U32, name="w2_codes%d%d" % (h, a), align_bytes=64)
-            plane = keep.tile([P, HALF], U8, name="w2_plane%d%d" % (h, a), align_bytes=64)
-            quantize(codes, plane, w2_grouped[h, a], 0, HALF)
-            for m in range(TILES):
-                product(h, m, a, 2, slice(0, HALF), codes[:].bitcast(FP8X4), plane[:], stop=(a == PASSES - 1))
-
-        pre = {}
-        res = [keep.tile([P, TILES, HALF], F32, name="res%d" % h) for h in range(2)]
-        out_tiles = out.rearrange("(m p) n -> p m n", p=P)
-
-        def add_bias(h, m):
-            s = keep.tile([P, HALF], F32, name="pre%d%d" % (h, m))
-            pre[h, m] = s
-            nc.vector.tensor_tensor(out=s[:], in0=acc[h, m][:], in1=bias[:, h * HALF : (h + 1) * HALF], op=ADD)
-
-        def silu(h, m):
-            nc.scalar.activation(out=res[h][:, m, :], in_=pre[h, m][:], func=SILU)
-
-        def store(h, m0, m1):
-            nc.sync.dma_start(out=out_tiles[:, m0:m1, h * HALF : (h + 1) * HALF], in_=res[h][:, m0:m1, :])
-
-        for a in range(PASSES - 1):
-            prepare_x(a)
-            packed_taps(a, (0, 1))
-        prepare_x(PASSES - 1)
-        packed_taps(PASSES - 1, (0,))
-        for a in range(PASSES):
-            cast_w2(0, a)
-            finish_w2(0, a)
-        packed_taps(PASSES - 1, (1,))
-
-        cast_w2(1, 0)
-        add_bias(0, 0)
-        finish_w2(1, 0)
-        add_bias(0, 1)
-        silu(0, 0)
-        cast_w2(1, 1)
-        add_bias(0, 2)
-        finish_w2(1, 1)
-        silu(0, 1)
-        store(0, 0, 2)
-        cast_w2(1, 2)
-        add_bias(0, 3)
-        finish_w2(1, 2)
-        silu(0, 2)
-        silu(0, 3)
-        store(0, 2, 4)
-        for m in range(TILES):
-            add_bias(1, m)
-            silu(1, m)
-            store(1, m, m + 1)
+        prepare_x(0)
+        products(0, 0, start=True)
+        products(0, 1)
+        prepare_x(1)
+        products(1, 0)
+        prepare_x(2)
+        products(2, 0)
+        prepare_w2(0)
+        products(0, 2)
+        prepare_w2(1)
+        for pc in pieces[:3]:
+            product(pc, 1, 2)
+        prepare_w2(2)
+        for a in (1, 2):
+            for pc in pieces[:2]:
+                product(pc, a, 1)
+        for pc in pieces[:2]:
+            product(pc, 2, 2, stop=True)
+            finish(pc)
+        for pc in pieces[2:]:
+            if pc[0] == TILES - 1:
+                product(pc, 1, 2)
+            product(pc, 1, 1)
+            product(pc, 2, 1)
+            product(pc, 2, 2, stop=True)
+            finish(pc)

from contextlib import ExitStack

import concourse.mybir as mybir
from concourse.masks import make_identity

D, K, M, T = 64, 1536, 512, 512
FLOPS = 2 * 3 * K * M * T

F32 = mybir.dt.float32
BF16 = mybir.dt.bfloat16
I32 = mybir.dt.int32
U32 = mybir.dt.uint32
U8 = mybir.dt.uint8
FP8X4 = mybir.dt.float8_e4m3fn_x4
FP4X4 = mybir.dt.float4_e2m1fn_x4
SILU = mybir.ActivationFunctionType.Silu
ADD = mybir.AluOpType.add

P = 128
PACK = 4
K_PASS = P * PACK
PASSES = K // K_PASS
XW = T + 2 * D
TILES = T // P
HALF = M // 2
N_FP4 = 128
X_CHUNKS = ((0, 256), (256, 384), (384, 640))
W2_VECTOR = ((0, 128), (128, 256), (256, 288))
W2_SCALAR = ((288, 384), (384, 512))


def interleave(copy, grouped, raw, c0, c1):
    dst = grouped[:, PACK * c0 : PACK * c1].rearrange("p (c i t) -> p c t i", i=4, t=PACK)
    src = raw[:, :, c0:c1].rearrange("p t (c i) -> p c t i", i=4)
    copy(out=dst, in_=src)


def tile_mix_dconv_tm_silu_kernel(tc, x, w0_words, w0_scales, w1_words, w1_scales, w2, b, out):
    nc = tc.nc
    with ExitStack() as ctx:
        keep = ctx.enter_context(tc.tile_pool(name="keep", bufs=1))
        psum = ctx.enter_context(tc.psum_pool(name="psum", bufs=1))
        ctx.enter_context(tc.manual_schedule())

        b_col = keep.tile([P, PACK], F32, name="b_col")
        nc.scalar.dma_start(out=b_col[:], in_=b.rearrange("(p c) -> p c", c=PACK))

        x_raw = [keep.tile([P, PACK, XW], F32, name="x_raw%d" % a) for a in range(PASSES)]
        w2_raw = [keep.tile([P, PACK, M], F32, name="w2_raw%d" % a) for a in range(PASSES)]
        w0_codes = keep.tile([P, PASSES * 2 * M], U8, name="w0_codes", align_bytes=64)
        w1_codes = [keep.tile([P, M], U32, name="w1_codes%d" % a, align_bytes=64) for a in range(PASSES)]
        w0_plane = keep.tile([P, PASSES * M], U8, name="w0_plane", align_bytes=64)
        w1_plane = keep.tile([P, PASSES * M], U8, name="w1_plane", align_bytes=64)

        def rows(t, a):
            return t[a * K_PASS : (a + 1) * K_PASS, :].rearrange("(p j) w -> p j w", j=PACK)

        def load_scales(plane, scales):
            nc.vector.memset(plane[:].bitcast(I32), 0)
            by_row = scales.bitcast(I32).rearrange("a (q r) n -> r q a n", r=4)
            for r in range(4):
                nc.sync.dma_start(
                    out=plane[r:P:32, :].bitcast(I32).rearrange("q (a n) -> q a n", a=PASSES),
                    in_=by_row[r],
                )

        def load_w1(a):
            nc.sync.dma_start(
                out=w1_codes[a][:].bitcast(I32), in_=w1_words[a].rearrange("p n t -> p (n t)").bitcast(I32)
            )

        ident = keep.tile([P, P], F32, name="ident")
        make_identity(nc, ident[:])

        nc.sync.dma_start(out=x_raw[0][:], in_=rows(x, 0))
        nc.sync.dma_start(
            out=w0_codes[:].bitcast(I32).rearrange("p (a n) -> p a n", a=PASSES),
            in_=w0_words.rearrange("a p n -> p a n").bitcast(I32),
        )
        load_scales(w0_plane, w0_scales)
        load_w1(0)
        nc.sync.dma_start(out=x_raw[1][:], in_=rows(x, 1))
        load_scales(w1_plane, w1_scales)
        nc.sync.dma_start(out=x_raw[2][:], in_=rows(x, 2))
        for a in range(PASSES):
            nc.sync.dma_start(out=w2_raw[a][:], in_=rows(w2, a))
        for a in range(1, PASSES):
            load_w1(a)

        warm = keep.tile([P, 8], F32, name="warm")
        nc.scalar.activation(out=warm[:], in_=ident[:, 0:8], func=SILU)

        spread = psum.tile([P, PACK, P], F32, name="spread")
        for c in range(PACK):
            nc.tensor.transpose(spread[:, c, :], b_col[:, c : c + 1].to_broadcast([P, P]), ident[:])
        bias = keep.tile([P, M], F32, name="bias")
        nc.scalar.copy(out=bias[:].rearrange("j (p c) -> j p c", c=PACK), in_=spread[:].rearrange("j c p -> j p c"))

        pieces = [(m, 0, M) for m in range(TILES - 1)] + [(TILES - 1, 0, HALF), (TILES - 1, HALF, HALF)]
        acc = {}
        for pc in pieces:
            acc[pc] = psum.tile([P, pc[2]], F32, name="acc%d_%d" % pc[:2])

        x_codes = [keep.tile([P, XW], U32, name="x_codes%d" % a, align_bytes=64) for a in range(PASSES)]
        x_plane = [keep.tile([P, XW], U8, name="x_plane%d" % a, align_bytes=64) for a in range(PASSES)]
        w2_codes = [keep.tile([P, M], U32, name="w2_codes%d" % a, align_bytes=64) for a in range(PASSES)]
        w2_plane = [keep.tile([P, M], U8, name="w2_plane%d" % a, align_bytes=64) for a in range(PASSES)]

        def quantize(codes, plane, grouped, c0, c1):
            nc.vector.quantize_mx(
                out=codes[:, c0:c1].bitcast(FP8X4), scales=plane[:, c0:c1], in_=grouped[:, PACK * c0 : PACK * c1]
            )

        def prepare_x(a):
            grouped = keep.tile([P, PACK * XW], BF16, name="x_grouped%d" % a, align_bytes=64)
            interleave(nc.vector.tensor_copy, grouped, x_raw[a], *X_CHUNKS[0])
            interleave(nc.vector.tensor_copy, grouped, x_raw[a], *X_CHUNKS[1])
            interleave(nc.scalar.copy, grouped, x_raw[a], *X_CHUNKS[2])
            for c0, c1 in X_CHUNKS:
                quantize(x_codes[a], x_plane[a], grouped, c0, c1)

        def prepare_w2(a):
            grouped = keep.tile([P, PACK * M], BF16, name="w2_grouped%d" % a, align_bytes=64)
            for c0, c1 in W2_SCALAR:
                interleave(nc.scalar.copy, grouped, w2_raw[a], c0, c1)
            interleave(nc.vector.tensor_copy, grouped, w2_raw[a], *W2_VECTOR[0])
            interleave(nc.vector.tensor_copy, grouped, w2_raw[a], *W2_VECTOR[1])
            quantize(w2_codes[a], w2_plane[a], grouped, 0, 128)
            interleave(nc.vector.tensor_copy, grouped, w2_raw[a], *W2_VECTOR[2])
            for c0 in range(128, M, 128):
                quantize(w2_codes[a], w2_plane[a], grouped, c0, c0 + 128)

        def product(pc, a, tap, start=False, stop=False):
            m, c0, width = pc
            t0 = tap * D + m * P
            step = N_FP4 if tap == 0 and width < M else width
            for q in range(0, width, step):
                n0 = c0 + q
                if tap == 0:
                    rhs = w0_codes[:, 2 * (a * M + n0) : 2 * (a * M + n0 + step)].bitcast(FP4X4)
                    rhs_scale = w0_plane[:, a * M + n0 : a * M + n0 + step]
                elif tap == 1:
                    rhs = w1_codes[a][:, n0 : n0 + step].bitcast(FP8X4)
                    rhs_scale = w1_plane[:, a * M + n0 : a * M + n0 + step]
                else:
                    rhs = w2_codes[a][:, n0 : n0 + step].bitcast(FP8X4)
                    rhs_scale = w2_plane[a][:, n0 : n0 + step]
                nc.tensor.matmul_mx(
                    out=acc[pc][:, q : q + step],
                    lhsT=x_codes[a][:, t0 : t0 + P].bitcast(FP8X4),
                    lhsT_scale=x_plane[a][:, t0 : t0 + P],
                    rhs=rhs,
                    rhs_scale=rhs_scale,
                    start=start and q == 0,
                    stop=stop,
                )

        def products(a, tap, start=False):
            for pc in pieces:
                product(pc, a, tap, start=start)

        def finish(pc):
            m, c0, width = pc
            pre = keep.tile([P, width], F32, name="pre%d_%d" % pc[:2])
            res = keep.tile([P, width], F32, name="res%d_%d" % pc[:2])
            nc.vector.tensor_tensor(out=pre[:], in0=acc[pc][:], in1=bias[:, c0 : c0 + width], op=ADD)
            nc.scalar.activation(out=res[:], in_=pre[:], func=SILU)
            nc.sync.dma_start(out=out[m * P : (m + 1) * P, c0 : c0 + width], in_=res[:])

        prepare_x(0)
        products(0, 0, start=True)
        products(0, 1)
        prepare_x(1)
        products(1, 0)
        prepare_x(2)
        products(2, 0)
        prepare_w2(0)
        products(0, 2)
        prepare_w2(1)
        for pc in pieces[:3]:
            product(pc, 1, 2)
        prepare_w2(2)
        for a in (1, 2):
            for pc in pieces[:2]:
                product(pc, a, 1)
        for pc in pieces[:2]:
            product(pc, 2, 2, stop=True)
            finish(pc)
        for pc in pieces[2:]:
            if pc[0] == TILES - 1:
                product(pc, 1, 2)
            product(pc, 1, 1)
            product(pc, 2, 1)
            product(pc, 2, 2, stop=True)
            finish(pc)
